import numpy as np
import ml_dtypes


def mxq(x, axis, fmt="e4m3"):
    dtype, down = {"e4m3": (ml_dtypes.float8_e4m3fn, 7), "e5m2": (ml_dtypes.float8_e5m2, 14)}[fmt]
    v = np.moveaxis(np.asarray(x, np.float32).astype(ml_dtypes.bfloat16).astype(np.float64), axis, -1)
    blocks = v.reshape(v.shape[:-1] + (-1, 32))
    amax = np.abs(blocks).max(-1, keepdims=True)
    byte = np.maximum(np.where(amax > 0, np.frexp(amax)[1] - 1 + 127, 0) - down, 1)
    scale = np.exp2(byte - 127.0)
    codes = (blocks / scale).astype(np.float32).astype(dtype).astype(np.float64)
    return np.moveaxis((codes * scale).reshape(v.shape), -1, axis)


WIDE = False


def mx_kscale(k):
    if not WIDE:
        return np.ones(k)
    levels = np.array([10, -10, 5, -5, 0])
    if k % 512:
        return np.exp2(np.random.permutation(np.resize(levels, k // 32))).repeat(32)
    a = np.empty((k // 512, 16))
    for p in range(k // 512):
        a[p, :8] = np.random.permutation(np.resize(levels, 8))
        for g in range(8):
            far = levels[np.abs(levels - a[p, g]) >= 10]
            a[p, g + 8] = far[np.random.randint(len(far))]
    return np.exp2(a.ravel()).repeat(32)


def f64(x):
    return np.asarray(x).astype(np.float64)


def striped(idx):
    return np.tile(idx.reshape(-1, 16).T, (8, 1)).astype(np.uint16)


def unstriped(offs):
    return offs[:16].T.reshape(-1).astype(np.int64)


E2M1 = np.array([0.0, 0.5, 1.0, 1.5, 2.0, 3.0, 4.0, 6.0, -0.0, -0.5, -1.0, -1.5, -2.0, -3.0, -4.0, -6.0])


def pack_weight(w, fmt):
    k, n = w.shape
    w = f64(np.asarray(w, np.float32).astype(ml_dtypes.bfloat16)).reshape(k // 32, 32, n)
    amax = np.abs(w).max(1)
    if fmt == "e4m3":
        byte = np.frexp(amax)[1] - 1 + 127 - 7
    else:
        mant, ex = np.frexp(amax / 6.0)
        byte = np.where(mant > 0.5, ex, ex - 1) + 127
    byte = np.clip(np.where(amax > 0, byte, 1), 1, 254)
    scaled = (w * np.exp2(127.0 - byte)[:, None, :]).reshape(k, n).astype(np.float32)
    by_word = np.ascontiguousarray(scaled.reshape(k // 512, 128, 4, n).transpose(0, 1, 3, 2))
    if fmt == "e4m3":
        words = by_word.astype(ml_dtypes.float8_e4m3fn).view(np.uint8)
    else:
        c = by_word.astype(ml_dtypes.float4_e2m1fn).view(np.uint8) & 0xF
        words = (c[..., 0::2] | (c[..., 1::2] << 4)).reshape(k // 512, 128, 2 * n)
    return np.ascontiguousarray(words), np.ascontiguousarray(byte.astype(np.uint8).reshape(k // 512, 16, n))


def unpack_weight(words, scales, fmt):
    g, _, n = scales.shape
    words = np.ascontiguousarray(words).reshape(g, 128, n, -1)
    if fmt == "e4m3":
        vals = words.view(ml_dtypes.float8_e4m3fn).astype(np.float64)
    else:
        nib = np.empty((g, 128, n, 4), np.uint8)
        nib[..., 0::2] = words & 0xF
        nib[..., 1::2] = words >> 4
        vals = E2M1[nib]
    vals = vals * np.repeat(np.exp2(scales.astype(np.float64) - 127.0), 8, axis=1)[..., None]
    return vals.transpose(0, 1, 3, 2).reshape(g * 512, n)


def silu(v):
    return v / (1.0 + np.exp(-np.maximum(v, -700.0)))


K, T, E, C, N = 1024, 1024, 16, 128, 128
TOP = 4
PAD = 64
K8 = 512


def by_expert(wq, xq):
    return np.concatenate([wq[e].T @ xq[:, e * C:(e + 1) * C] for e in range(E)], axis=1)


def setup_inputs():
    n = np.random.standard_normal
    s = mx_kscale(K)[:, None]
    slot_token = np.empty(E * C, np.int64); pos = np.tile(E * C + np.arange(T) % PAD, (TOP, 1)); taken = np.zeros(T, np.int64)
    liked = np.random.randn(T)
    for e in np.random.permutation(E):
        free = np.flatnonzero(taken < TOP); pick = np.random.permutation(free[np.argsort(-(liked[free] + np.random.gumbel(size=free.size)))[:C]]); slot_token[e * C:(e + 1) * C] = pick
        pos[taken[pick], pick] = e * C + np.arange(C); taken[pick] += 1
    g = np.random.uniform(0.2, 0.8, (TOP, T))
    w = n((E, K, N)) / np.sqrt(K) / s[None]
    w8 = [pack_weight(m[:K8], "e4m3") for m in w]
    w4 = [pack_weight(m[K8:], "e2m1") for m in w]
    return {
        "xT": (n((K, T)) * s).astype(np.float32),
        "w8_words": np.stack([m[0] for m in w8]),
        "w8_scales": np.stack([m[1] for m in w8]),
        "w4_words": np.stack([m[0] for m in w4]),
        "w4_scales": np.stack([m[1] for m in w4]),
        "b": (0.3 * n((N, E))).astype(np.float32),
        "gate": np.stack([np.tile(r, (N, 1)) for r in g]).astype(np.float32),
        "offs": striped(slot_token),
        "pos1": striped(pos[0]),
        "pos2": striped(pos[1]),
        "pos3": striped(pos[2]),
        "pos4": striped(pos[3]),
    }


def reference(xT, w8_words, w8_scales, w4_words, w4_scales, b, gate, offs, pos1, pos2, pos3, pos4):
    idx = unstriped(offs)
    w = np.stack([np.concatenate([unpack_weight(w8_words[e], w8_scales[e], "e4m3"), unpack_weight(w4_words[e], w4_scales[e], "e2m1")]) for e in range(E)])
    xq = mxq(f64(xT)[:, idx], 0, "e4m3")
    y = by_expert(w, xq)
    y = silu(y + np.repeat(f64(b), C, axis=1))
    y = np.concatenate([y, np.zeros((N, PAD))], axis=1)
    return sum(f64(gate[r]) * y[:, unstriped(p)] for r, p in enumerate((pos1, pos2, pos3, pos4)))

@@ -1,0 +1,213 @@
+from contextlib import ExitStack
+
+import concourse.mybir as mybir
+from concourse.masks import make_identity
+
+K, T, E, C, N = 1024, 1024, 16, 128, 128
+TOP = 4
+PAD = 64
+S = E * C
+FLOPS = 2 * K * N * S
+
+F32 = mybir.dt.float32
+BF16 = mybir.dt.bfloat16
+I32 = mybir.dt.int32
+U32 = mybir.dt.uint32
+U16 = mybir.dt.uint16
+U8 = mybir.dt.uint8
+FP8X4 = mybir.dt.float8_e4m3fn_x4
+FP4X4 = mybir.dt.float4_e2m1fn_x4
+ACT = mybir.ActivationFunctionType
+ALU = mybir.AluOpType
+
+P = 128
+PACK = 4
+K_PASS = P * PACK
+LIST = 16
+FP8_ROW = 4
+FIRST_CHUNKS = (512, 256, 256)
+SECOND_CHUNKS = (256, 256, 256, 256)
+GROUP = 4
+HALF = T // 2
+BLOCKS = T // P
+
+
+def runs(sizes):
+    out, at = [], 0
+    for size in sizes:
+        out.append((at, at + size))
+        at += size
+    return out
+
+
+def tile_moe_ecr_lin_silu_kernel(
+    tc, xT, w8_words, w8_scales, w4_words, w4_scales, b, gate, offs, pos1, pos2, pos3, pos4, out
+):
+    nc = tc.nc
+    with ExitStack() as ctx:
+        keep = ctx.enter_context(tc.tile_pool(name="keep", bufs=1))
+        ring = ctx.enter_context(tc.tile_pool(name="ring", bufs=8))
+        work = ctx.enter_context(tc.psum_pool(name="work", bufs=6))
+        sums = ctx.enter_context(tc.psum_pool(name="sums", bufs=1))
+
+        x_scales = keep.tile([P, T], U8, name="x_scales", align_bytes=64)
+        nc.vector.memset(x_scales[:].bitcast(I32), 0)
+        w_scales = keep.tile([P, S], U8, name="w_scales", align_bytes=64)
+        nc.vector.memset(w_scales[:].bitcast(I32), 0)
+        y = keep.tile([P, S + PAD], F32, name="y")
+        nc.vector.memset(y[:, S:], 0.0)
+        gate_rows = keep.tile([P, P], F32, name="gate_rows")
+        nc.gpsimd.memset(gate_rows[:], 0.0)
+        ident = keep.tile([P, P], F32, name="ident")
+        make_identity(nc, ident[:])
+
+        def load_x(k0, sizes, name):
+            rows = xT[k0:k0 + K_PASS, :].rearrange("(p j) t -> p j t", j=PACK)
+            tiles = []
+            for i, (t0, t1) in enumerate(runs(sizes)):
+                raw = keep.tile([P, PACK, t1 - t0], F32, name="%s_raw%d" % (name, i))
+                nc.sync.dma_start(out=raw[:], in_=rows[:, :, t0:t1])
+                tiles.append(raw)
+            return tiles
+
+        raw4 = load_x(K_PASS, FIRST_CHUNKS, "x4")
+        slots = keep.tile([P, S // LIST], U16, name="slots")
+        nc.sync.dma_start(slots[:], offs)
+        raw8 = load_x(0, SECOND_CHUNKS, "x8")
+
+        scale_words = w_scales[:].bitcast(I32).rearrange("p (e n) -> p e n", e=E)
+        for row0, src in ((0, w4_scales), (FP8_ROW, w8_scales)):
+            for r in range(4):
+                nc.sync.dma_start(
+                    out=scale_words[row0 + r:P:32],
+                    in_=src[:, 0, r:16:4, :].bitcast(I32).rearrange("e q n -> q e n"),
+                )
+        bias = keep.tile([P, E], F32, name="bias")
+        nc.sync.dma_start(out=bias[:], in_=b)
+        w4, w8 = [], []
+        for g in range(E // GROUP):
+            experts = slice(g * GROUP, (g + 1) * GROUP)
+            t4 = keep.tile([P, GROUP, 2 * N], U8, name="w4_%d" % g, align_bytes=64)
+            nc.sync.dma_start(
+                out=t4[:].bitcast(I32), in_=w4_words[experts, 0].bitcast(I32).rearrange("e p n -> p e n")
+            )
+            t8 = keep.tile([P, GROUP, 4 * N], U8, name="w8_%d" % g, align_bytes=64)
+            nc.sync.dma_start(
+                out=t8[:].bitcast(I32),
+                in_=w8_words[experts, 0].rearrange("e p n r -> e p (n r)").bitcast(I32).rearrange("e p n -> p e n"),
+            )
+            w4.append(t4)
+            w8.append(t8)
+        for r in range(TOP):
+            nc.sync.dma_start(
+                out=gate_rows[r * BLOCKS:(r + 1) * BLOCKS, :], in_=gate[r, 0, :].rearrange("(b t) -> b t", t=P)
+            )
+        gate_last = keep.tile([P, HALF], F32, name="gate_last")
+        nc.sync.dma_start(out=gate_last[:], in_=gate[TOP - 1, :, HALF:])
+        places = []
+        for r, src in enumerate((pos1, pos2, pos3, pos4)):
+            place = keep.tile([P, T // LIST], U16, name="place%d" % r)
+            nc.sync.dma_start(place[:], src)
+            places.append(place)
+
+        def interleave(engine_copy, grouped, raw, c0, c1):
+            engine_copy(
+                grouped[:, c0:c1, :].rearrange("p (c i) j -> p c j i", i=4),
+                raw[:, :, c0:c1].rearrange("p j (c i) -> p c j i", i=4),
+            )
+
+        def scalar_copy(dst, src):
+            nc.scalar.activation(dst, src, ACT.Copy)
+
+        def quantise(raws, sizes, vector_eighths, words, row0, name):
+            for i, (t0, t1) in enumerate(runs(sizes)):
+                width = t1 - t0
+                grouped = keep.tile([P, width, PACK], BF16, name="%s_bf%d" % (name, i), align_bytes=64)
+                cut = width * vector_eighths // 8
+                if cut > 0:
+                    interleave(nc.vector.tensor_copy, grouped, raws[i], 0, cut)
+                interleave(scalar_copy, grouped, raws[i], cut, width)
+                nc.vector.quantize_mx(
+                    out=words[:, t0:t1].bitcast(FP8X4),
+                    scales=x_scales[row0:P, t0:t1],
+                    in_=grouped[:].rearrange("p t j -> p (t j)"),
+                )
+
+        def gather(dst, window, offsets, a, z):
+            nc.vector.tensor_copy(dst, window[:].indirect(offsets[:, a // LIST:z // LIST]))
+
+        x4_words = keep.tile([P, T], U32, name="x4_words", align_bytes=64)
+        x8_words = keep.tile([P, T], U32, name="x8_words", align_bytes=64)
+        s4_words = keep.tile([P, S], U32, name="s4_words", align_bytes=64)
+        s8_words = keep.tile([P, S], U32, name="s8_words", align_bytes=64)
+        s_scales = keep.tile([P, S], U8, name="s_scales", align_bytes=64)
+
+        quantise(raw4, FIRST_CHUNKS, 5, x4_words, 0, "x4")
+        for a, z in runs((768, 768, 512)):
+            gather(s4_words[:, a:z], x4_words, slots, a, z)
+        quantise(raw8, SECOND_CHUNKS, 0, x8_words, FP8_ROW, "x8")
+
+        def expert(e):
+            cols = slice(e * C, (e + 1) * C)
+            g, m = divmod(e, GROUP)
+            acc = work.tile([P, C], F32, name="acc", tag="work")
+            nc.tensor.matmul_mx(
+                out=acc[:], lhsT=w4[g][:, m, :].bitcast(FP4X4), lhsT_scale=w_scales[:, cols],
+                rhs=s4_words[:, cols].bitcast(FP8X4), rhs_scale=s_scales[:, cols], start=True, stop=False,
+            )
+            nc.tensor.matmul_mx(
+                out=acc[:], lhsT=w8[g][:, m, :].bitcast(FP8X4), lhsT_scale=w_scales[FP8_ROW:P, cols],
+                rhs=s8_words[:, cols].bitcast(FP8X4), rhs_scale=s_scales[FP8_ROW:P, cols], start=False, stop=True,
+            )
+            nc.scalar.activation(y[:, cols], acc[:], ACT.Silu, bias=bias[:, e:e + 1])
+
+        for (a, z), word_runs in zip(runs((768, 768, 512)), ((768,), (768,), (384, 128))):
+            gather(s_scales[:, a:z], x_scales, slots, a, z)
+            for c0, c1 in runs(word_runs):
+                gather(s8_words[:, a + c0:a + c1], x8_words, slots, a + c0, a + c1)
+                for e in range((a + c0) // C, (a + c1) // C):
+                    expert(e)
+
+        gate_t = work.tile([P, P], F32, name="gate_t", tag="work")
+        nc.tensor.transpose(gate_t[:], gate_rows[:], ident[:])
+        gate_cols = keep.tile([P, TOP * BLOCKS], F32, name="gate_cols")
+        nc.scalar.activation(gate_cols[:], gate_t[:, 0:TOP * BLOCKS], ACT.Copy)
+
+        totals = [sums.tile([P, HALF], F32, name="total%d" % h) for h in range(2)]
+        order = [(0, 1), (1, 1), (0, 0), (1, 0), (2, 1), (2, 0), (3, 0)]
+        last = {0: TOP - 1, 1: TOP - 2}
+        for r, h in order:
+            fetched = keep.tile([P, HALF], F32, name="fetched%d_%d" % (r, h))
+            gather(fetched[:], y, places[r], h * HALF, (h + 1) * HALF)
+            scaled_tiles = []
+            for i in range(HALF // P):
+                turned = work.tile([P, P], F32, name="turned", tag="work")
+                nc.tensor.transpose(turned[:], fetched[:, i * P:(i + 1) * P], ident[:])
+                col = r * BLOCKS + h * (HALF // P) + i
+                scaled = ring.tile([P, P], F32, name="scaled")
+                nc.scalar.activation(scaled[:], turned[:], ACT.Copy, scale=gate_cols[:, col:col + 1])
+                scaled_tiles.append(scaled)
+            for i in range(HALF // P):
+                nc.tensor.matmul(
+                    totals[h][:, i * P:(i + 1) * P], scaled_tiles[i][:], ident[:], is_transpose=True,
+                    start=(r == 0 and i == 0), stop=(r == last[h] and i == HALF // P - 1),
+                )
+        result0 = keep.tile([P, HALF], F32, name="result0")
+        nc.scalar.activation(result0[:], totals[0][:], ACT.Copy)
+        nc.scalar.dma_start(out=out[:, 0:HALF], in_=result0[:])
+
+        quarter = HALF // 2
+        products = []
+        for q in range(2):
+            product = keep.tile([P, quarter], F32, name="product%d" % q)
+            t0 = HALF + q * quarter
+            nc.vector.tensor_tensor(
+                product[:], y[:].indirect(places[TOP - 1][:, t0 // LIST:(t0 + quarter) // LIST]),
+                gate_last[:, q * quarter:(q + 1) * quarter], ALU.mult,
+            )
+            products.append(product)
+        for q in range(2):
+            result = keep.tile([P, quarter], F32, name="result1_%d" % q)
+            nc.vector.tensor_tensor(result[:], totals[1][:, q * quarter:(q + 1) * quarter], products[q][:], ALU.add)
+            t0 = HALF + q * quarter
+            nc.sync.dma_start(out=out[:, t0:t0 + quarter], in_=result[:])

@@ -29,7 +29,7 @@ FIRST_CHUNKS = (512, 256, 256)
 SECOND_CHUNKS = (256, 256, 256, 256)
 GROUP = 4
 HALF = T // 2
-BLOCKS = T // P
+PARTS = (512, 256, 256)
 
 
 def runs(sizes):
@@ -46,9 +46,7 @@ def tile_moe_ecr_lin_silu_kernel(
     nc = tc.nc
     with ExitStack() as ctx:
         keep = ctx.enter_context(tc.tile_pool(name="keep", bufs=1))
-        ring = ctx.enter_context(tc.tile_pool(name="ring", bufs=8))
-        work = ctx.enter_context(tc.psum_pool(name="work", bufs=6))
-        sums = ctx.enter_context(tc.psum_pool(name="sums", bufs=1))
+        psum = ctx.enter_context(tc.psum_pool(name="psum", bufs=8))
 
         x_scales = keep.tile([P, T], U8, name="x_scales", align_bytes=64)
         nc.vector.memset(x_scales[:].bitcast(I32), 0)
@@ -56,8 +54,6 @@ def tile_moe_ecr_lin_silu_kernel(
         nc.vector.memset(w_scales[:].bitcast(I32), 0)
         y = keep.tile([P, S + PAD], F32, name="y")
         nc.vector.memset(y[:, S:], 0.0)
-        gate_rows = keep.tile([P, P], F32, name="gate_rows")
-        nc.gpsimd.memset(gate_rows[:], 0.0)
         ident = keep.tile([P, P], F32, name="ident")
         make_identity(nc, ident[:])
 
@@ -98,17 +94,18 @@ def tile_moe_ecr_lin_silu_kernel(
             )
             w4.append(t4)
             w8.append(t8)
-        for r in range(TOP):
-            nc.sync.dma_start(
-                out=gate_rows[r * BLOCKS:(r + 1) * BLOCKS, :], in_=gate[r, 0, :].rearrange("(b t) -> b t", t=P)
-            )
-        gate_last = keep.tile([P, HALF], F32, name="gate_last")
-        nc.sync.dma_start(out=gate_last[:], in_=gate[TOP - 1, :, HALF:])
         places = []
         for r, src in enumerate((pos1, pos2, pos3, pos4)):
             place = keep.tile([P, T // LIST], U16, name="place%d" % r)
             nc.sync.dma_start(place[:], src)
             places.append(place)
+        gates = {}
+        for a, z in runs(PARTS):
+            for r in range(TOP - 1):
+                gates[r, a] = keep.tile([P, z - a], F32, name="gate%d_%d" % (r, a))
+                nc.sync.dma_start(out=gates[r, a][:], in_=gate[r, :, a:z])
+        last_gate = keep.tile([P, T], F32, name="last_gate")
+        nc.sync.dma_start(out=last_gate[:], in_=gate[TOP - 1])
 
         def interleave(engine_copy, grouped, raw, c0, c1):
             engine_copy(
@@ -123,7 +120,7 @@ def tile_moe_ecr_lin_silu_kernel(
             for i, (t0, t1) in enumerate(runs(sizes)):
                 width = t1 - t0
                 grouped = keep.tile([P, width, PACK], BF16, name="%s_bf%d" % (name, i), align_bytes=64)
-                cut = width * vector_eighths // 8
+                cut = width * vector_eighths[i] // 8
                 if cut > 0:
                     interleave(nc.vector.tensor_copy, grouped, raws[i], 0, cut)
                 interleave(scalar_copy, grouped, raws[i], cut, width)
@@ -142,72 +139,81 @@ def tile_moe_ecr_lin_silu_kernel(
         s8_words = keep.tile([P, S], U32, name="s8_words", align_bytes=64)
         s_scales = keep.tile([P, S], U8, name="s_scales", align_bytes=64)
 
-        quantise(raw4, FIRST_CHUNKS, 5, x4_words, 0, "x4")
+        quantise(raw4, FIRST_CHUNKS, (5, 5, 5), x4_words, 0, "x4")
         for a, z in runs((768, 768, 512)):
             gather(s4_words[:, a:z], x4_words, slots, a, z)
-        quantise(raw8, SECOND_CHUNKS, 0, x8_words, FP8_ROW, "x8")
+        quantise(raw8, SECOND_CHUNKS, (0, 0, 0, 3), x8_words, FP8_ROW, "x8")
 
-        def expert(e):
+        def bank(name):
+            return psum.tile([P, HALF], F32, name=name, tag="bank")
+
+        sums = {}
+
+        def fp4_pass(e):
             cols = slice(e * C, (e + 1) * C)
             g, m = divmod(e, GROUP)
-            acc = work.tile([P, C], F32, name="acc", tag="work")
+            sums[e] = bank("acc")
             nc.tensor.matmul_mx(
-                out=acc[:], lhsT=w4[g][:, m, :].bitcast(FP4X4), lhsT_scale=w_scales[:, cols],
+                out=sums[e][:, 0:C], lhsT=w4[g][:, m, :].bitcast(FP4X4), lhsT_scale=w_scales[:, cols],
                 rhs=s4_words[:, cols].bitcast(FP8X4), rhs_scale=s_scales[:, cols], start=True, stop=False,
             )
+
+        def fp8_pass(e):
+            cols = slice(e * C, (e + 1) * C)
+            g, m = divmod(e, GROUP)
             nc.tensor.matmul_mx(
-                out=acc[:], lhsT=w8[g][:, m, :].bitcast(FP8X4), lhsT_scale=w_scales[FP8_ROW:P, cols],
+                out=sums[e][:, 0:C], lhsT=w8[g][:, m, :].bitcast(FP8X4), lhsT_scale=w_scales[FP8_ROW:P, cols],
                 rhs=s8_words[:, cols].bitcast(FP8X4), rhs_scale=s_scales[FP8_ROW:P, cols], start=False, stop=True,
             )
-            nc.scalar.activation(y[:, cols], acc[:], ACT.Silu, bias=bias[:, e:e + 1])
+            nc.scalar.activation(y[:, cols], sums[e][:, 0:C], ACT.Silu, bias=bias[:, e:e + 1])
 
-        for (a, z), word_runs in zip(runs((768, 768, 512)), ((768,), (768,), (384, 128))):
-            gather(s_scales[:, a:z], x_scales, slots, a, z)
-            for c0, c1 in runs(word_runs):
-                gather(s8_words[:, a + c0:a + c1], x8_words, slots, a + c0, a + c1)
-                for e in range((a + c0) // C, (a + c1) // C):
-                    expert(e)
+        e0 = 0
+        for word_runs in ((4,), (4,), (2, 2), (2,), (1, 1)):
+            e1 = e0 + sum(word_runs)
+            gather(s_scales[:, e0 * C:e1 * C], x_scales, slots, e0 * C, e1 * C)
+            for e in range(e0, e1):
+                fp4_pass(e)
+            for a, z in runs(word_runs):
+                a, z = e0 + a, e0 + z
+                gather(s8_words[:, a * C:z * C], x8_words, slots, a * C, z * C)
+                for e in range(a, z):
+                    fp8_pass(e)
+            e0 = e1
 
-        gate_t = work.tile([P, P], F32, name="gate_t", tag="work")
-        nc.tensor.transpose(gate_t[:], gate_rows[:], ident[:])
-        gate_cols = keep.tile([P, TOP * BLOCKS], F32, name="gate_cols")
-        nc.scalar.activation(gate_cols[:], gate_t[:, 0:TOP * BLOCKS], ACT.Copy)
+        def multiply(r, a, z, weights):
+            product = keep.tile([P, z - a], F32, name="product%d_%d" % (r, a))
+            nc.vector.tensor_tensor(product[:], y[:].indirect(places[r][:, a // LIST:z // LIST]), weights, ALU.mult)
+            return product
 
-        totals = [sums.tile([P, HALF], F32, name="total%d" % h) for h in range(2)]
-        order = [(0, 1), (1, 1), (0, 0), (1, 0), (2, 1), (2, 0), (3, 0)]
-        last = {0: TOP - 1, 1: TOP - 2}
-        for r, h in order:
-            fetched = keep.tile([P, HALF], F32, name="fetched%d_%d" % (r, h))
-            gather(fetched[:], y, places[r], h * HALF, (h + 1) * HALF)
-            scaled_tiles = []
-            for i in range(HALF // P):
-                turned = work.tile([P, P], F32, name="turned", tag="work")
-                nc.tensor.transpose(turned[:], fetched[:, i * P:(i + 1) * P], ident[:])
-                col = r * BLOCKS + h * (HALF // P) + i
-                scaled = ring.tile([P, P], F32, name="scaled")
-                nc.scalar.activation(scaled[:], turned[:], ACT.Copy, scale=gate_cols[:, col:col + 1])
-                scaled_tiles.append(scaled)
-            for i in range(HALF // P):
-                nc.tensor.matmul(
-                    totals[h][:, i * P:(i + 1) * P], scaled_tiles[i][:], ident[:], is_transpose=True,
-                    start=(r == 0 and i == 0), stop=(r == last[h] and i == HALF // P - 1),
-                )
-        result0 = keep.tile([P, HALF], F32, name="result0")
-        nc.scalar.activation(result0[:], totals[0][:], ACT.Copy)
-        nc.scalar.dma_start(out=out[:, 0:HALF], in_=result0[:])
+        totals = []
+        for a, z in runs(PARTS):
+            blocks = [slice(c, c + P) for c in range(0, z - a, P)]
+            turned = bank("turned")
+            for r in range(TOP - 1):
+                product = multiply(r, a, z, gates[r, a][:])
+                for i, cols in enumerate(blocks):
+                    nc.tensor.matmul(
+                        turned[:, cols], product[:, cols], ident[:], is_transpose=True,
+                        start=(r == 0 and i == 0), stop=(r == TOP - 2 and i == len(blocks) - 1),
+                    )
+            summed = keep.tile([P, z - a], F32, name="summed%d" % a)
+            nc.scalar.activation(summed[:], turned[:, 0:z - a], ACT.Copy)
+            total = bank("total")
+            for cols in blocks:
+                nc.tensor.transpose(total[:, cols], summed[:, cols], ident[:])
+            totals.append(total)
 
-        quarter = HALF // 2
-        products = []
-        for q in range(2):
-            product = keep.tile([P, quarter], F32, name="product%d" % q)
-            t0 = HALF + q * quarter
-            nc.vector.tensor_tensor(
-                product[:], y[:].indirect(places[TOP - 1][:, t0 // LIST:(t0 + quarter) // LIST]),
-                gate_last[:, q * quarter:(q + 1) * quarter], ALU.mult,
-            )
-            products.append(product)
-        for q in range(2):
-            result = keep.tile([P, quarter], F32, name="result1_%d" % q)
-            nc.vector.tensor_tensor(result[:], totals[1][:, q * quarter:(q + 1) * quarter], products[q][:], ALU.add)
-            t0 = HALF + q * quarter
-            nc.sync.dma_start(out=out[:, t0:t0 + quarter], in_=result[:])
+        lasts = []
+
+        def finish(i):
+            a, z = runs(PARTS)[i]
+            result = keep.tile([P, z - a], F32, name="result%d" % a)
+            nc.vector.tensor_tensor(result[:], totals[i][:, 0:z - a], lasts[i][:], ALU.add)
+            queue = nc.scalar if i == len(PARTS) - 1 else nc.sync
+            queue.dma_start(out=out[:, a:z], in_=result[:])
+
+        for i, (a, z) in enumerate(runs(PARTS)):
+            lasts.append(multiply(TOP - 1, a, z, last_gate[:, a:z]))
+            if i > 0:
+                finish(i - 1)
+        finish(len(PARTS) - 1)

@@ -27,7 +27,7 @@ LIST = 16
 FP8_ROW = 4
 FIRST_CHUNKS = (512, 256, 256)
 SECOND_CHUNKS = (256, 256, 256, 256)
-GROUP = 4
+GROUPS = (4, 4, 4, 2, 2)
 HALF = T // 2
 PARTS = (512, 256, 256)
 
@@ -81,29 +81,33 @@ def tile_moe_ecr_lin_silu_kernel(
         bias = keep.tile([P, E], F32, name="bias")
         nc.sync.dma_start(out=bias[:], in_=b)
         w4, w8 = [], []
-        for g in range(E // GROUP):
-            experts = slice(g * GROUP, (g + 1) * GROUP)
-            t4 = keep.tile([P, GROUP, 2 * N], U8, name="w4_%d" % g, align_bytes=64)
+        for e0, e1 in runs(GROUPS):
+            t4 = keep.tile([P, e1 - e0, 2 * N], U8, name="w4_%d" % e0, align_bytes=64)
             nc.sync.dma_start(
-                out=t4[:].bitcast(I32), in_=w4_words[experts, 0].bitcast(I32).rearrange("e p n -> p e n")
+                out=t4[:].bitcast(I32), in_=w4_words[e0:e1, 0].bitcast(I32).rearrange("e p n -> p e n")
             )
-            t8 = keep.tile([P, GROUP, 4 * N], U8, name="w8_%d" % g, align_bytes=64)
+            t8 = keep.tile([P, e1 - e0, 4 * N], U8, name="w8_%d" % e0, align_bytes=64)
             nc.sync.dma_start(
                 out=t8[:].bitcast(I32),
-                in_=w8_words[experts, 0].rearrange("e p n r -> e p (n r)").bitcast(I32).rearrange("e p n -> p e n"),
+                in_=w8_words[e0:e1, 0].rearrange("e p n r -> e p (n r)").bitcast(I32).rearrange("e p n -> p e n"),
             )
-            w4.append(t4)
-            w8.append(t8)
-        places = []
-        for r, src in enumerate((pos1, pos2, pos3, pos4)):
-            place = keep.tile([P, T // LIST], U16, name="place%d" % r)
+            w4.extend(t4[:, m, :].bitcast(FP4X4) for m in range(e1 - e0))
+            w8.extend(t8[:, m, :].bitcast(FP8X4) for m in range(e1 - e0))
+
+        places, gates = [], {}
+
+        def load_places(src):
+            place = keep.tile([P, T // LIST], U16, name="place%d" % len(places))
             nc.sync.dma_start(place[:], src)
             places.append(place)
-        gates = {}
-        for a, z in runs(PARTS):
-            for r in range(TOP - 1):
+
+        for i, (a, z) in enumerate(runs(PARTS)):
+            for r, src in enumerate((pos1, pos2, pos3)):
+                if i == 0:
+                    load_places(src)
                 gates[r, a] = keep.tile([P, z - a], F32, name="gate%d_%d" % (r, a))
                 nc.sync.dma_start(out=gates[r, a][:], in_=gate[r, :, a:z])
+        load_places(pos4)
         last_gate = keep.tile([P, T], F32, name="last_gate")
         nc.sync.dma_start(out=last_gate[:], in_=gate[TOP - 1])
 
@@ -139,10 +143,10 @@ def tile_moe_ecr_lin_silu_kernel(
         s8_words = keep.tile([P, S], U32, name="s8_words", align_bytes=64)
         s_scales = keep.tile([P, S], U8, name="s_scales", align_bytes=64)
 
-        quantise(raw4, FIRST_CHUNKS, (5, 5, 5), x4_words, 0, "x4")
+        quantise(raw4, FIRST_CHUNKS, (5, 5, 6), x4_words, 0, "x4")
         for a, z in runs((768, 768, 512)):
             gather(s4_words[:, a:z], x4_words, slots, a, z)
-        quantise(raw8, SECOND_CHUNKS, (0, 0, 0, 3), x8_words, FP8_ROW, "x8")
+        quantise(raw8, SECOND_CHUNKS, (0, 0, 0, 2), x8_words, FP8_ROW, "x8")
 
         def bank(name):
             return psum.tile([P, HALF], F32, name=name, tag="bank")
@@ -151,24 +155,22 @@ def tile_moe_ecr_lin_silu_kernel(
 
         def fp4_pass(e):
             cols = slice(e * C, (e + 1) * C)
-            g, m = divmod(e, GROUP)
             sums[e] = bank("acc")
             nc.tensor.matmul_mx(
-                out=sums[e][:, 0:C], lhsT=w4[g][:, m, :].bitcast(FP4X4), lhsT_scale=w_scales[:, cols],
+                out=sums[e][:, 0:C], lhsT=w4[e], lhsT_scale=w_scales[:, cols],
                 rhs=s4_words[:, cols].bitcast(FP8X4), rhs_scale=s_scales[:, cols], start=True, stop=False,
             )
 
         def fp8_pass(e):
             cols = slice(e * C, (e + 1) * C)
-            g, m = divmod(e, GROUP)
             nc.tensor.matmul_mx(
-                out=sums[e][:, 0:C], lhsT=w8[g][:, m, :].bitcast(FP8X4), lhsT_scale=w_scales[FP8_ROW:P, cols],
+                out=sums[e][:, 0:C], lhsT=w8[e], lhsT_scale=w_scales[FP8_ROW:P, cols],
                 rhs=s8_words[:, cols].bitcast(FP8X4), rhs_scale=s_scales[FP8_ROW:P, cols], start=False, stop=True,
             )
             nc.scalar.activation(y[:, cols], sums[e][:, 0:C], ACT.Silu, bias=bias[:, e:e + 1])
 
         e0 = 0
-        for word_runs in ((4,), (4,), (2, 2), (2,), (1, 1)):
+        for word_runs in ((6,), (3, 3), (2,), (1, 1)):
             e1 = e0 + sum(word_runs)
             gather(s_scales[:, e0 * C:e1 * C], x_scales, slots, e0 * C, e1 * C)
             for e in range(e0, e1):

from contextlib import ExitStack

import concourse.mybir as mybir
from concourse.masks import make_identity

K, T, E, C, N = 1024, 1024, 16, 128, 128
TOP = 4
PAD = 64
S = E * C
FLOPS = 2 * K * N * S

F32 = mybir.dt.float32
BF16 = mybir.dt.bfloat16
I32 = mybir.dt.int32
U32 = mybir.dt.uint32
U16 = mybir.dt.uint16
U8 = mybir.dt.uint8
FP8X4 = mybir.dt.float8_e4m3fn_x4
FP4X4 = mybir.dt.float4_e2m1fn_x4
ACT = mybir.ActivationFunctionType
ALU = mybir.AluOpType

P = 128
PACK = 4
K_PASS = P * PACK
LIST = 16
FP8_ROW = 4
FIRST_CHUNKS = (512, 256, 256)
SECOND_CHUNKS = (256, 256, 256, 256)
GROUPS = (4, 4, 4, 2, 2)
HALF = T // 2
PARTS = (512, 256, 256)


def runs(sizes):
    out, at = [], 0
    for size in sizes:
        out.append((at, at + size))
        at += size
    return out


def tile_moe_ecr_lin_silu_kernel(
    tc, xT, w8_words, w8_scales, w4_words, w4_scales, b, gate, offs, pos1, pos2, pos3, pos4, out
):
    nc = tc.nc
    with ExitStack() as ctx:
        keep = ctx.enter_context(tc.tile_pool(name="keep", bufs=1))
        psum = ctx.enter_context(tc.psum_pool(name="psum", bufs=8))

        x_scales = keep.tile([P, T], U8, name="x_scales", align_bytes=64)
        nc.vector.memset(x_scales[:].bitcast(I32), 0)
        w_scales = keep.tile([P, S], U8, name="w_scales", align_bytes=64)
        nc.vector.memset(w_scales[:].bitcast(I32), 0)
        y = keep.tile([P, S + PAD], F32, name="y")
        nc.vector.memset(y[:, S:], 0.0)
        ident = keep.tile([P, P], F32, name="ident")
        make_identity(nc, ident[:])

        def load_x(k0, sizes, name):
            rows = xT[k0:k0 + K_PASS, :].rearrange("(p j) t -> p j t", j=PACK)
            tiles = []
            for i, (t0, t1) in enumerate(runs(sizes)):
                raw = keep.tile([P, PACK, t1 - t0], F32, name="%s_raw%d" % (name, i))
                nc.sync.dma_start(out=raw[:], in_=rows[:, :, t0:t1])
                tiles.append(raw)
            return tiles

        raw4 = load_x(K_PASS, FIRST_CHUNKS, "x4")
        slots = keep.tile([P, S // LIST], U16, name="slots")
        nc.sync.dma_start(slots[:], offs)
        raw8 = load_x(0, SECOND_CHUNKS, "x8")

        scale_words = w_scales[:].bitcast(I32).rearrange("p (e n) -> p e n", e=E)
        for row0, src in ((0, w4_scales), (FP8_ROW, w8_scales)):
            for r in range(4):
                nc.sync.dma_start(
                    out=scale_words[row0 + r:P:32],
                    in_=src[:, 0, r:16:4, :].bitcast(I32).rearrange("e q n -> q e n"),
                )
        bias = keep.tile([P, E], F32, name="bias")
        nc.sync.dma_start(out=bias[:], in_=b)
        w4, w8 = [], []
        for e0, e1 in runs(GROUPS):
            t4 = keep.tile([P, e1 - e0, 2 * N], U8, name="w4_%d" % e0, align_bytes=64)
            nc.sync.dma_start(
                out=t4[:].bitcast(I32), in_=w4_words[e0:e1, 0].bitcast(I32).rearrange("e p n -> p e n")
            )
            t8 = keep.tile([P, e1 - e0, 4 * N], U8, name="w8_%d" % e0, align_bytes=64)
            nc.sync.dma_start(
                out=t8[:].bitcast(I32),
                in_=w8_words[e0:e1, 0].rearrange("e p n r -> e p (n r)").bitcast(I32).rearrange("e p n -> p e n"),
            )
            w4.extend(t4[:, m, :].bitcast(FP4X4) for m in range(e1 - e0))
            w8.extend(t8[:, m, :].bitcast(FP8X4) for m in range(e1 - e0))

        places, gates = [], {}

        def load_places(src):
            place = keep.tile([P, T // LIST], U16, name="place%d" % len(places))
            nc.sync.dma_start(place[:], src)
            places.append(place)

        for i, (a, z) in enumerate(runs(PARTS)):
            for r, src in enumerate((pos1, pos2, pos3)):
                if i == 0:
                    load_places(src)
                gates[r, a] = keep.tile([P, z - a], F32, name="gate%d_%d" % (r, a))
                nc.sync.dma_start(out=gates[r, a][:], in_=gate[r, :, a:z])
        load_places(pos4)
        last_gate = keep.tile([P, T], F32, name="last_gate")
        nc.sync.dma_start(out=last_gate[:], in_=gate[TOP - 1])

        def interleave(engine_copy, grouped, raw, c0, c1):
            engine_copy(
                grouped[:, c0:c1, :].rearrange("p (c i) j -> p c j i", i=4),
                raw[:, :, c0:c1].rearrange("p j (c i) -> p c j i", i=4),
            )

        def scalar_copy(dst, src):
            nc.scalar.activation(dst, src, ACT.Copy)

        def quantise(raws, sizes, vector_eighths, words, row0, name):
            for i, (t0, t1) in enumerate(runs(sizes)):
                width = t1 - t0
                grouped = keep.tile([P, width, PACK], BF16, name="%s_bf%d" % (name, i), align_bytes=64)
                cut = width * vector_eighths[i] // 8
                if cut > 0:
                    interleave(nc.vector.tensor_copy, grouped, raws[i], 0, cut)
                interleave(scalar_copy, grouped, raws[i], cut, width)
                nc.vector.quantize_mx(
                    out=words[:, t0:t1].bitcast(FP8X4),
                    scales=x_scales[row0:P, t0:t1],
                    in_=grouped[:].rearrange("p t j -> p (t j)"),
                )

        def gather(dst, window, offsets, a, z):
            nc.vector.tensor_copy(dst, window[:].indirect(offsets[:, a // LIST:z // LIST]))

        x4_words = keep.tile([P, T], U32, name="x4_words", align_bytes=64)
        x8_words = keep.tile([P, T], U32, name="x8_words", align_bytes=64)
        s4_words = keep.tile([P, S], U32, name="s4_words", align_bytes=64)
        s8_words = keep.tile([P, S], U32, name="s8_words", align_bytes=64)
        s_scales = keep.tile([P, S], U8, name="s_scales", align_bytes=64)

        quantise(raw4, FIRST_CHUNKS, (5, 5, 6), x4_words, 0, "x4")
        for a, z in runs((768, 768, 512)):
            gather(s4_words[:, a:z], x4_words, slots, a, z)
        quantise(raw8, SECOND_CHUNKS, (0, 0, 0, 2), x8_words, FP8_ROW, "x8")

        def bank(name):
            return psum.tile([P, HALF], F32, name=name, tag="bank")

        sums = {}

        def fp4_pass(e):
            cols = slice(e * C, (e + 1) * C)
            sums[e] = bank("acc")
            nc.tensor.matmul_mx(
                out=sums[e][:, 0:C], lhsT=w4[e], lhsT_scale=w_scales[:, cols],
                rhs=s4_words[:, cols].bitcast(FP8X4), rhs_scale=s_scales[:, cols], start=True, stop=False,
            )

        def fp8_pass(e):
            cols = slice(e * C, (e + 1) * C)
            nc.tensor.matmul_mx(
                out=sums[e][:, 0:C], lhsT=w8[e], lhsT_scale=w_scales[FP8_ROW:P, cols],
                rhs=s8_words[:, cols].bitcast(FP8X4), rhs_scale=s_scales[FP8_ROW:P, cols], start=False, stop=True,
            )
            nc.scalar.activation(y[:, cols], sums[e][:, 0:C], ACT.Silu, bias=bias[:, e:e + 1])

        e0 = 0
        for word_runs in ((6,), (3, 3), (2,), (1, 1)):
            e1 = e0 + sum(word_runs)
            gather(s_scales[:, e0 * C:e1 * C], x_scales, slots, e0 * C, e1 * C)
            for e in range(e0, e1):
                fp4_pass(e)
            for a, z in runs(word_runs):
                a, z = e0 + a, e0 + z
                gather(s8_words[:, a * C:z * C], x8_words, slots, a * C, z * C)
                for e in range(a, z):
                    fp8_pass(e)
            e0 = e1

        def multiply(r, a, z, weights):
            product = keep.tile([P, z - a], F32, name="product%d_%d" % (r, a))
            nc.vector.tensor_tensor(product[:], y[:].indirect(places[r][:, a // LIST:z // LIST]), weights, ALU.mult)
            return product

        totals = []
        for a, z in runs(PARTS):
            blocks = [slice(c, c + P) for c in range(0, z - a, P)]
            turned = bank("turned")
            for r in range(TOP - 1):
                product = multiply(r, a, z, gates[r, a][:])
                for i, cols in enumerate(blocks):
                    nc.tensor.matmul(
                        turned[:, cols], product[:, cols], ident[:], is_transpose=True,
                        start=(r == 0 and i == 0), stop=(r == TOP - 2 and i == len(blocks) - 1),
                    )
            summed = keep.tile([P, z - a], F32, name="summed%d" % a)
            nc.scalar.activation(summed[:], turned[:, 0:z - a], ACT.Copy)
            total = bank("total")
            for cols in blocks:
                nc.tensor.transpose(total[:, cols], summed[:, cols], ident[:])
            totals.append(total)

        lasts = []

        def finish(i):
            a, z = runs(PARTS)[i]
            result = keep.tile([P, z - a], F32, name="result%d" % a)
            nc.vector.tensor_tensor(result[:], totals[i][:, 0:z - a], lasts[i][:], ALU.add)
            queue = nc.scalar if i == len(PARTS) - 1 else nc.sync
            queue.dma_start(out=out[:, a:z], in_=result[:])

        for i, (a, z) in enumerate(runs(PARTS)):
            lasts.append(multiply(TOP - 1, a, z, last_gate[:, a:z]))
            if i > 0:
                finish(i - 1)
        finish(len(PARTS) - 1)
